import numpy as np
import ml_dtypes

BF16 = ml_dtypes.bfloat16


def bf(x):
    return np.asarray(x, np.float32).astype(BF16)


def f32(x):
    return np.asarray(x, np.float32)


def f64(x):
    return np.asarray(x).astype(np.float64)


def striped(idx):
    return np.tile(idx.reshape(-1, 16).T, (8, 1))


def rows(idx, k):
    return np.tile(idx, (k, 1))


def look(tab, idx):
    return np.take_along_axis(f64(tab), rows(idx, len(tab)), axis=1)


K, S, D, V, N = 256, 2048, 2, 1024, 2048


def setup_inputs():
    return {"tab": bf(0.7 * np.random.standard_normal((D, K, S))), "base": bf(np.random.standard_normal((K, V))), "offs": striped(np.random.randint(0, S, N))}


def reference(tab, base, offs):
    idx = offs[:16].T.reshape(-1)
    x = f64(base) + sum(look(tab[d], idx[d * V:(d + 1) * V]) for d in range(D))
    return x

@@ -1,0 +1,43 @@
+import concourse.mybir as mybir
+
+F32, BF16, U16 = mybir.dt.float32, mybir.dt.bfloat16, mybir.dt.uint16
+P = 128
+LANES = 16
+
+
+def tile_lookup_res_add_out_kernel(tc, tab, base, offs, out):
+    nc = tc.nc
+    add = mybir.AluOpType.add
+    stages, rows, codewords = tab.shape
+    vectors = base.shape[1]
+    columns = vectors // LANES
+
+    with (
+        tc.tile_pool(name="held", bufs=1) as held,
+        tc.tile_pool(name="loaded", bufs=4) as loaded,
+        tc.tile_pool(name="windows", bufs=4) as windows,
+        tc.tile_pool(name="sums", bufs=2) as sums,
+    ):
+        offsets = held.tile([P, stages * columns], U16, name="offsets")
+        nc.sync.dma_start(offsets[:], offs)
+
+        for first_row in range(0, rows, P):
+            block = slice(first_row, first_row + P)
+
+            base_loaded = loaded.tile([P, vectors], BF16, name="base_loaded")
+            nc.scalar.dma_start(base_loaded[:], base[block, :])
+            total = sums.tile([P, vectors], F32, name="total_0")
+            nc.vector.tensor_copy(total[:], base_loaded[:])
+
+            for d in range(stages):
+                codebook = loaded.tile([P, codewords], BF16, name="codebook")
+                nc.sync.dma_start(codebook[:], tab[d, block, :])
+                window = windows.tile([P, codewords], F32, name="window")
+                nc.scalar.copy(window[:], codebook[:])
+
+                picks = window[:].indirect(offsets[:, d * columns : (d + 1) * columns])
+                new_total = sums.tile([P, vectors], F32, name=f"total_{d + 1}")
+                nc.vector.tensor_tensor(new_total[:], picks, total[:], add)
+                total = new_total
+
+            nc.sync.dma_start(out[block, :], total[:])

@@ -5,39 +5,51 @@ P = 128
 LANES = 16
 
 
+def halves(length):
+    return slice(0, length // 2), slice(length // 2, length)
+
+
 def tile_lookup_res_add_out_kernel(tc, tab, base, offs, out):
     nc = tc.nc
     add = mybir.AluOpType.add
     stages, rows, codewords = tab.shape
     vectors = base.shape[1]
-    columns = vectors // LANES
+    blocks = [slice(r, r + P) for r in range(0, rows, P)]
 
-    with (
-        tc.tile_pool(name="held", bufs=1) as held,
-        tc.tile_pool(name="loaded", bufs=4) as loaded,
-        tc.tile_pool(name="windows", bufs=4) as windows,
-        tc.tile_pool(name="sums", bufs=2) as sums,
-    ):
-        offsets = held.tile([P, stages * columns], U16, name="offsets")
+    with tc.tile_pool(name="held", bufs=1) as held:
+        offsets = held.tile([P, stages * vectors // LANES], U16, name="offsets")
+        base_f32 = [held.tile([P, vectors], F32, name=f"base_f32_{b}") for b in range(len(blocks))]
+
+        def load_base(b):
+            raw = held.tile([P, vectors], BF16, name=f"base_{b}")
+            nc.sync.dma_start(raw[:], base[blocks[b], :])
+            nc.scalar.copy(base_f32[b][:], raw[:])
+
+        def load_window(d, b, cast):
+            raw = held.tile([P, codewords], BF16, name=f"codebook_{d}_{b}")
+            window = held.tile([P, codewords], F32, name=f"window_{d}_{b}")
+            for half in halves(codewords):
+                nc.sync.dma_start(raw[:, half], tab[d, blocks[b], half])
+                cast(window[:, half], raw[:, half])
+            return window
+
+        def look_up_and_add(total, window, d, entries, plain):
+            first = (d * vectors + entries.start) // LANES
+            last = (d * vectors + entries.stop) // LANES
+            picks = window[:].indirect(offsets[:, first:last])
+            nc.vector.tensor_tensor(total[:, entries], picks, plain[:, entries], add)
+
+        load_base(0)
         nc.sync.dma_start(offsets[:], offs)
+        load_base(1)
+        windows = {(0, 0): load_window(0, 0, nc.vector.tensor_copy)}
+        for d, b in ((1, 0), (0, 1), (1, 1)):
+            windows[d, b] = load_window(d, b, nc.scalar.copy)
 
-        for first_row in range(0, rows, P):
-            block = slice(first_row, first_row + P)
-
-            base_loaded = loaded.tile([P, vectors], BF16, name="base_loaded")
-            nc.scalar.dma_start(base_loaded[:], base[block, :])
-            total = sums.tile([P, vectors], F32, name="total_0")
-            nc.vector.tensor_copy(total[:], base_loaded[:])
-
-            for d in range(stages):
-                codebook = loaded.tile([P, codewords], BF16, name="codebook")
-                nc.sync.dma_start(codebook[:], tab[d, block, :])
-                window = windows.tile([P, codewords], F32, name="window")
-                nc.scalar.copy(window[:], codebook[:])
-
-                picks = window[:].indirect(offsets[:, d * columns : (d + 1) * columns])
-                new_total = sums.tile([P, vectors], F32, name=f"total_{d + 1}")
-                nc.vector.tensor_tensor(new_total[:], picks, total[:], add)
-                total = new_total
-
-            nc.sync.dma_start(out[block, :], total[:])
+        for b, block in enumerate(blocks):
+            first_sum = held.tile([P, vectors], F32, name=f"first_sum_{b}")
+            look_up_and_add(first_sum, windows[0, b], 0, slice(0, vectors), base_f32[b])
+            result = held.tile([P, vectors], F32, name=f"result_{b}")
+            for half in halves(vectors):
+                look_up_and_add(result, windows[1, b], 1, half, first_sum)
+                nc.sync.dma_start(out[block, half], result[:, half])

@@ -15,41 +15,48 @@ def tile_lookup_res_add_out_kernel(tc, tab, base, offs, out):
     stages, rows, codewords = tab.shape
     vectors = base.shape[1]
     blocks = [slice(r, r + P) for r in range(0, rows, P)]
+    pairs = [(d, b) for b in range(len(blocks)) for d in range(stages)]
 
     with tc.tile_pool(name="held", bufs=1) as held:
         offsets = held.tile([P, stages * vectors // LANES], U16, name="offsets")
+        base_raw = [held.tile([P, vectors], BF16, name=f"base_raw_{b}") for b in range(len(blocks))]
         base_f32 = [held.tile([P, vectors], F32, name=f"base_f32_{b}") for b in range(len(blocks))]
+        codebook = {(d, b): held.tile([P, codewords], BF16, name=f"codebook_{d}_{b}") for d, b in pairs}
+        window = {(d, b): held.tile([P, codewords], F32, name=f"window_{d}_{b}") for d, b in pairs}
 
-        def load_base(b):
-            raw = held.tile([P, vectors], BF16, name=f"base_{b}")
-            nc.sync.dma_start(raw[:], base[blocks[b], :])
-            nc.scalar.copy(base_f32[b][:], raw[:])
-
-        def load_window(d, b, cast):
-            raw = held.tile([P, codewords], BF16, name=f"codebook_{d}_{b}")
-            window = held.tile([P, codewords], F32, name=f"window_{d}_{b}")
+        for d, b in pairs:
+            if d == 0:
+                nc.sync.dma_start(base_raw[b][:], base[blocks[b], :])
             for half in halves(codewords):
-                nc.sync.dma_start(raw[:, half], tab[d, blocks[b], half])
-                cast(window[:, half], raw[:, half])
-            return window
+                nc.sync.dma_start(codebook[d, b][:, half], tab[d, blocks[b], half])
+            if (d, b) == pairs[0]:
+                nc.sync.dma_start(offsets[:], offs)
 
-        def look_up_and_add(total, window, d, entries, plain):
+        for d, b in pairs:
+            if d == 0:
+                half = halves(vectors)[0]
+                nc.scalar.copy(base_f32[b][:, half], base_raw[b][:, half])
+            if (d, b) != pairs[0]:
+                for half in halves(codewords):
+                    nc.scalar.copy(window[d, b][:, half], codebook[d, b][:, half])
+
+        def look_up_and_add(total, d, b, entries, plain):
             first = (d * vectors + entries.start) // LANES
             last = (d * vectors + entries.stop) // LANES
-            picks = window[:].indirect(offsets[:, first:last])
+            picks = window[d, b][:].indirect(offsets[:, first:last])
             nc.vector.tensor_tensor(total[:, entries], picks, plain[:, entries], add)
 
-        load_base(0)
-        nc.sync.dma_start(offsets[:], offs)
-        load_base(1)
-        windows = {(0, 0): load_window(0, 0, nc.vector.tensor_copy)}
-        for d, b in ((1, 0), (0, 1), (1, 1)):
-            windows[d, b] = load_window(d, b, nc.scalar.copy)
-
+        whole = slice(0, vectors)
         for b, block in enumerate(blocks):
+            half = halves(vectors)[1]
+            nc.vector.tensor_copy(base_f32[b][:, half], base_raw[b][:, half])
+            if b == 0:
+                for half in halves(codewords):
+                    nc.vector.tensor_copy(window[pairs[0]][:, half], codebook[pairs[0]][:, half])
+
             first_sum = held.tile([P, vectors], F32, name=f"first_sum_{b}")
-            look_up_and_add(first_sum, windows[0, b], 0, slice(0, vectors), base_f32[b])
+            look_up_and_add(first_sum, 0, b, whole, base_f32[b])
             result = held.tile([P, vectors], F32, name=f"result_{b}")
-            for half in halves(vectors):
-                look_up_and_add(result, windows[1, b], 1, half, first_sum)
-                nc.sync.dma_start(out[block, half], result[:, half])
+            for entries in halves(vectors) if block == blocks[-1] else [whole]:
+                look_up_and_add(result, 1, b, entries, first_sum)
+                nc.sync.dma_start(out[block, entries], result[:, entries])

import concourse.mybir as mybir

F32, BF16, U16 = mybir.dt.float32, mybir.dt.bfloat16, mybir.dt.uint16
P = 128
LANES = 16


def halves(length):
    return slice(0, length // 2), slice(length // 2, length)


def tile_lookup_res_add_out_kernel(tc, tab, base, offs, out):
    nc = tc.nc
    add = mybir.AluOpType.add
    stages, rows, codewords = tab.shape
    vectors = base.shape[1]
    blocks = [slice(r, r + P) for r in range(0, rows, P)]
    pairs = [(d, b) for b in range(len(blocks)) for d in range(stages)]

    with tc.tile_pool(name="held", bufs=1) as held:
        offsets = held.tile([P, stages * vectors // LANES], U16, name="offsets")
        base_raw = [held.tile([P, vectors], BF16, name=f"base_raw_{b}") for b in range(len(blocks))]
        base_f32 = [held.tile([P, vectors], F32, name=f"base_f32_{b}") for b in range(len(blocks))]
        codebook = {(d, b): held.tile([P, codewords], BF16, name=f"codebook_{d}_{b}") for d, b in pairs}
        window = {(d, b): held.tile([P, codewords], F32, name=f"window_{d}_{b}") for d, b in pairs}

        for d, b in pairs:
            if d == 0:
                nc.sync.dma_start(base_raw[b][:], base[blocks[b], :])
            for half in halves(codewords):
                nc.sync.dma_start(codebook[d, b][:, half], tab[d, blocks[b], half])
            if (d, b) == pairs[0]:
                nc.sync.dma_start(offsets[:], offs)

        for d, b in pairs:
            if d == 0:
                half = halves(vectors)[0]
                nc.scalar.copy(base_f32[b][:, half], base_raw[b][:, half])
            if (d, b) != pairs[0]:
                for half in halves(codewords):
                    nc.scalar.copy(window[d, b][:, half], codebook[d, b][:, half])

        def look_up_and_add(total, d, b, entries, plain):
            first = (d * vectors + entries.start) // LANES
            last = (d * vectors + entries.stop) // LANES
            picks = window[d, b][:].indirect(offsets[:, first:last])
            nc.vector.tensor_tensor(total[:, entries], picks, plain[:, entries], add)

        whole = slice(0, vectors)
        for b, block in enumerate(blocks):
            half = halves(vectors)[1]
            nc.vector.tensor_copy(base_f32[b][:, half], base_raw[b][:, half])
            if b == 0:
                for half in halves(codewords):
                    nc.vector.tensor_copy(window[pairs[0]][:, half], codebook[pairs[0]][:, half])

            first_sum = held.tile([P, vectors], F32, name=f"first_sum_{b}")
            look_up_and_add(first_sum, 0, b, whole, base_f32[b])
            result = held.tile([P, vectors], F32, name=f"result_{b}")
            for entries in halves(vectors) if block == blocks[-1] else [whole]:
                look_up_and_add(result, 1, b, entries, first_sum)
                nc.sync.dma_start(out[block, entries], result[:, entries])
